import numpy as np
import ml_dtypes


def mxq(x, axis, fmt="e4m3"):
    dtype, down = {"e4m3": (ml_dtypes.float8_e4m3fn, 7), "e5m2": (ml_dtypes.float8_e5m2, 14)}[fmt]
    v = np.moveaxis(np.asarray(x, np.float32).astype(ml_dtypes.bfloat16).astype(np.float64), axis, -1)
    blocks = v.reshape(v.shape[:-1] + (-1, 32))
    amax = np.abs(blocks).max(-1, keepdims=True)
    byte = np.maximum(np.where(amax > 0, np.frexp(amax)[1] - 1 + 127, 0) - down, 1)
    scale = np.exp2(byte - 127.0)
    codes = (blocks / scale).astype(np.float32).astype(dtype).astype(np.float64)
    return np.moveaxis((codes * scale).reshape(v.shape), -1, axis)


WIDE = False


def mx_kscale(k):
    if not WIDE:
        return np.ones(k)
    levels = np.array([10, -10, 5, -5, 0])
    if k % 512:
        return np.exp2(np.random.permutation(np.resize(levels, k // 32))).repeat(32)
    a = np.empty((k // 512, 16))
    for p in range(k // 512):
        a[p, :8] = np.random.permutation(np.resize(levels, 8))
        for g in range(8):
            far = levels[np.abs(levels - a[p, g]) >= 10]
            a[p, g + 8] = far[np.random.randint(len(far))]
    return np.exp2(a.ravel()).repeat(32)


def f64(x):
    return np.asarray(x).astype(np.float64)


def striped8(idx):
    return np.asarray(idx).reshape(8, -1, 16).transpose(0, 2, 1).reshape(128, -1).astype(np.uint16)


def unstriped8(offs):
    return offs.reshape(8, 16, -1).transpose(0, 2, 1).reshape(8, -1).astype(np.int64)


def pick8(x, idx, run):
    r = np.arange(len(x))
    return x[r[:, None], idx[r % (8 * run) // run]]


E2M1 = np.array([0.0, 0.5, 1.0, 1.5, 2.0, 3.0, 4.0, 6.0, -0.0, -0.5, -1.0, -1.5, -2.0, -3.0, -4.0, -6.0])


def pack_weight(w, fmt):
    k, n = w.shape
    w = f64(np.asarray(w, np.float32).astype(ml_dtypes.bfloat16)).reshape(k // 32, 32, n)
    amax = np.abs(w).max(1)
    if fmt == "e4m3":
        byte = np.frexp(amax)[1] - 1 + 127 - 7
    else:
        mant, ex = np.frexp(amax / 6.0)
        byte = np.where(mant > 0.5, ex, ex - 1) + 127
    byte = np.clip(np.where(amax > 0, byte, 1), 1, 254)
    scaled = (w * np.exp2(127.0 - byte)[:, None, :]).reshape(k, n).astype(np.float32)
    by_word = np.ascontiguousarray(scaled.reshape(k // 512, 128, 4, n).transpose(0, 1, 3, 2))
    if fmt == "e4m3":
        words = by_word.astype(ml_dtypes.float8_e4m3fn).view(np.uint8)
    else:
        c = by_word.astype(ml_dtypes.float4_e2m1fn).view(np.uint8) & 0xF
        words = (c[..., 0::2] | (c[..., 1::2] << 4)).reshape(k // 512, 128, 2 * n)
    return np.ascontiguousarray(words), np.ascontiguousarray(byte.astype(np.uint8).reshape(k // 512, 16, n))


def unpack_weight(words, scales, fmt):
    g, _, n = scales.shape
    words = np.ascontiguousarray(words).reshape(g, 128, n, -1)
    if fmt == "e4m3":
        vals = words.view(ml_dtypes.float8_e4m3fn).astype(np.float64)
    else:
        nib = np.empty((g, 128, n, 4), np.uint8)
        nib[..., 0::2] = words & 0xF
        nib[..., 1::2] = words >> 4
        vals = E2M1[nib]
    vals = vals * np.repeat(np.exp2(scales.astype(np.float64) - 127.0), 8, axis=1)[..., None]
    return vals.transpose(0, 1, 3, 2).reshape(g * 512, n)


D, T, U, I, Q = 512, 1024, 1024, 512, 128


def setup_inputs():
    n = np.random.standard_normal
    idx = np.stack([np.random.permutation(T)[:I] for _ in range(8)])
    idx2 = np.stack([np.random.permutation(U)[:I] for _ in range(8)])
    idx3 = np.stack([np.random.permutation(T)[:I] for _ in range(8)])
    idx4 = np.stack([np.random.permutation(U)[:I] for _ in range(8)])
    idx5 = np.stack([np.random.permutation(T)[:I] for _ in range(8)])
    fd = mx_kscale(D)
    keysp = pack_weight(n((D, T)) / fd[:, None], "e2m1")
    notesp = pack_weight(n((D, U)) / fd[:, None], "e4m3")
    return {
        "query": (n((D, Q)) * 1.0 / np.sqrt(D) * fd[:, None]).astype(np.float32),
        "keys_words": keysp[0],
        "keys_scales": keysp[1],
        "notes_words": notesp[0],
        "notes_scales": notesp[1],
        "lam": (np.random.uniform(0.3, 0.7, (Q, 1))).astype(np.float32),
        "offs": striped8(idx),
        "offs2": striped8(idx2),
        "offs3": striped8(idx3),
        "offs4": striped8(idx4),
        "offs5": striped8(idx5),
    }


def reference(query, keys_words, keys_scales, notes_words, notes_scales, lam, offs, offs2, offs3, offs4, offs5):
    idx = unstriped8(offs)
    idx2 = unstriped8(offs2)
    idx3 = unstriped8(offs3)
    idx4 = unstriped8(offs4)
    idx5 = unstriped8(offs5)
    keysu = unpack_weight(keys_words, keys_scales, "e2m1")
    notesu = unpack_weight(notes_words, notes_scales, "e4m3")
    queryq = mxq(f64(query), 0, "e4m3")
    a = queryq.T @ keysu
    b = queryq.T @ notesu
    r = pick8(a, idx, 16) - pick8(b, idx2, 16)
    f1 = np.zeros((Q, T))
    f1[np.arange(Q)[:, None], idx[np.arange(Q) % 128 // 16]] = r
    f2 = np.zeros((Q, U))
    f2[np.arange(Q)[:, None], idx2[np.arange(Q) % 128 // 16]] = r
    aa = a - f1 * f64(lam)
    bb = b + f2 * f64(lam)
    r2 = pick8(aa, idx3, 16) - pick8(bb, idx4, 16)
    f3 = np.zeros((Q, T))
    f3[np.arange(Q)[:, None], idx3[np.arange(Q) % 128 // 16]] = r2
    a3 = aa - f3 * f64(lam)
    y = pick8(a3, idx5, 16)
    return y

@@ -1,0 +1,140 @@
+from contextlib import ExitStack
+
+import concourse.mybir as mybir
+
+D, T, U, SLOTS, Q = 512, 1024, 1024, 512, 128
+FLOPS = 2 * D * Q * (T + U)
+
+F32 = mybir.dt.float32
+BF16 = mybir.dt.bfloat16
+I32 = mybir.dt.int32
+U32 = mybir.dt.uint32
+U16 = mybir.dt.uint16
+U8 = mybir.dt.uint8
+FP8X4 = mybir.dt.float8_e4m3fn_x4
+FP4X4 = mybir.dt.float4_e2m1fn_x4
+MULT = mybir.AluOpType.mult
+ADD = mybir.AluOpType.add
+SUB = mybir.AluOpType.subtract
+COPY = mybir.ActivationFunctionType.Copy
+
+P = 128
+PACK = 4
+BANK = 512
+HALF = SLOTS // 2
+LIST_COLS = SLOTS // 16
+LO = slice(0, HALF)
+HI = slice(HALF, SLOTS)
+LIST_LO = slice(0, LIST_COLS // 2)
+LIST_HI = slice(LIST_COLS // 2, LIST_COLS)
+
+
+def tile_attend_gossip_two_kernel(tc, query, keys_words, keys_scales, notes_words, notes_scales, lam,
+                                   offs, offs2, offs3, offs4, offs5, out):
+    nc = tc.nc
+    with ExitStack() as ctx:
+        lists = ctx.enter_context(tc.tile_pool(name="lists", bufs=1))
+        sb = ctx.enter_context(tc.tile_pool(name="sb", bufs=1))
+        psum = ctx.enter_context(tc.psum_pool(name="psum", bufs=1))
+
+        def load_list(name, src):
+            tile = lists.tile([P, LIST_COLS], U16, name=name)
+            nc.sync.dma_start(tile[:], src)
+            return tile
+
+        def load_scales(name, src, width):
+            plane = sb.tile([P, width], U8, name=name, align_bytes=64)
+            nc.vector.memset(plane[:].bitcast(I32), 0)
+            for quad in range(4):
+                nc.scalar.dma_start(plane[32 * quad : 32 * quad + 4, :].bitcast(I32),
+                                    src[0, 4 * quad : 4 * quad + 4, :].bitcast(I32))
+            return plane
+
+        q_raw = sb.tile([P, PACK, Q], F32, name="q_raw")
+        nc.sync.dma_start(q_raw[:], query.rearrange("(p j) q -> p j q", j=PACK))
+        n_scales = load_scales("n_scales", notes_scales, U)
+        n_words = sb.tile([P, U], U32, name="n_words", align_bytes=64)
+        nc.sync.dma_start(n_words[:].bitcast(I32), notes_words[0].rearrange("p n t -> p (n t)").bitcast(I32))
+        k_scales = load_scales("k_scales", keys_scales, T)
+        k_words = sb.tile([P, 2 * T], U8, name="k_words", align_bytes=64)
+        nc.sync.dma_start(k_words[:].bitcast(I32), keys_words[0].bitcast(I32))
+        idx2 = load_list("idx2", offs2)
+        idx = load_list("idx", offs)
+        lam_sb = sb.tile([P, 1], F32, name="lam_sb")
+        nc.sync.dma_start(lam_sb[:], lam)
+        idx4 = load_list("idx4", offs4)
+        idx3 = load_list("idx3", offs3)
+        idx5 = load_list("idx5", offs5)
+
+        f1 = sb.tile([P, T], F32, name="f1")
+        f2 = sb.tile([P, U], F32, name="f2")
+        f3 = sb.tile([P, T], F32, name="f3")
+        nc.vector.memset(f2[:], 0.0)
+        nc.vector.memset(f1[:], 0.0)
+
+        q_bf = sb.tile([P, Q, PACK], BF16, name="q_bf", align_bytes=64)
+        nc.vector.tensor_copy(q_bf[:], q_raw[:].rearrange("p j q -> p q j"))
+        q_codes = sb.tile([P, Q], U32, name="q_codes", align_bytes=64)
+        q_scales = sb.tile([P, Q], U8, name="q_scales", align_bytes=64)
+        nc.vector.quantize_mx(out=q_codes[:].bitcast(FP8X4), scales=q_scales[:],
+                              in_=q_bf[:].rearrange("p q j -> p (q j)"))
+        nc.vector.memset(f3[:], 0.0)
+
+        def scores(name, words, scales, width):
+            bank = psum.tile([P, width], F32, name=name)
+            nc.tensor.matmul_mx(out=bank[:], lhsT=q_codes[:].bitcast(FP8X4), lhsT_scale=q_scales[:],
+                                rhs=words, rhs_scale=scales, start=True, stop=True)
+            return bank
+
+        def key_scores(name, c0, c1):
+            return scores(name, k_words[:, 2 * c0 : 2 * c1].bitcast(FP4X4), k_scales[:, c0:c1], c1 - c0)
+
+        a = sb.tile([P, T], F32, name="a")
+        b = sb.tile([P, U], F32, name="b")
+        b0 = scores("b0", n_words[:, 0:BANK].bitcast(FP8X4), n_scales[:, 0:BANK], BANK)
+        b1 = scores("b1", n_words[:, BANK:U].bitcast(FP8X4), n_scales[:, BANK:U], BANK)
+        a0 = key_scores("a0", 0, 512)
+        a1 = key_scores("a1", 512, 768)
+        a2 = key_scores("a2", 768, 1024)
+        nc.scalar.copy(b[:, 0:BANK], b0[:])
+        nc.scalar.copy(b[:, BANK:U], b1[:])
+        nc.vector.tensor_copy(a[:, 0:512], a0[:])
+        gb = sb.tile([P, HALF], F32, name="gb")
+        nc.scalar.activation(gb[:], b[:].indirect(idx2[:, LIST_LO]), COPY)
+        nc.vector.tensor_copy(a[:, 512:768], a1[:])
+        nc.scalar.copy(a[:, 768:1024], a2[:])
+
+        r_lo = sb.tile([P, HALF], F32, name="r_lo")
+        nc.vector.tensor_tensor(r_lo[:], a[:].indirect(idx[:, LIST_LO]), gb[:], SUB)
+        ga_hi = sb.tile([P, HALF], F32, name="ga_hi")
+        ngb_hi = sb.tile([P, HALF], F32, name="ngb_hi")
+        nc.scalar.activation(ga_hi[:], a[:].indirect(idx[:, LIST_HI]), COPY)
+        nc.scalar.activation(ngb_hi[:], b[:].indirect(idx2[:, LIST_HI]), COPY, scale=-1.0)
+        neg_lam = sb.tile([P, 1], F32, name="neg_lam")
+        nc.scalar.activation(neg_lam[:], lam_sb[:], COPY, scale=-1.0)
+
+        nc.vector.tensor_copy(f2[:].indirect(idx2[:, LIST_LO]), r_lo[:])
+        nc.vector.tensor_copy(f1[:].indirect(idx[:, LIST_LO]), r_lo[:])
+        nc.vector.tensor_tensor(f2[:].indirect(idx2[:, LIST_HI]), ga_hi[:], ngb_hi[:], ADD)
+        nc.vector.tensor_tensor(f1[:].indirect(idx[:, LIST_HI]), ga_hi[:], ngb_hi[:], ADD)
+
+        aa = sb.tile([P, T], F32, name="aa")
+        bb = sb.tile([P, U], F32, name="bb")
+        nc.vector.scalar_tensor_tensor(bb[:], f2[:], lam_sb[:], b[:], MULT, ADD)
+        nc.vector.scalar_tensor_tensor(aa[:], f1[:], neg_lam[:], a[:], MULT, ADD)
+
+        ngbb = sb.tile([P, SLOTS], F32, name="ngbb")
+        gaa = sb.tile([P, SLOTS], F32, name="gaa")
+        nc.scalar.activation(ngbb[:], bb[:].indirect(idx4[:]), COPY, scale=-1.0)
+        nc.vector.tensor_copy(gaa[:, LO], aa[:].indirect(idx3[:, LIST_LO]))
+        nc.scalar.activation(gaa[:, HI], aa[:].indirect(idx3[:, LIST_HI]), COPY)
+        nc.vector.tensor_tensor(f3[:].indirect(idx3[:]), gaa[:], ngbb[:], ADD)
+
+        a3 = sb.tile([P, T], F32, name="a3")
+        nc.vector.scalar_tensor_tensor(a3[:], f3[:], neg_lam[:], aa[:], MULT, ADD)
+        y_lo = sb.tile([P, HALF], F32, name="y_lo")
+        y_hi = sb.tile([P, HALF], F32, name="y_hi")
+        nc.vector.tensor_copy(y_lo[:], a3[:].indirect(idx5[:, LIST_LO]))
+        nc.scalar.activation(y_hi[:], a3[:].indirect(idx5[:, LIST_HI]), COPY)
+        nc.sync.dma_start(out[:, LO], y_lo[:])
+        nc.scalar.dma_start(out[:, HI], y_hi[:])

@@ -46,17 +46,17 @@ def tile_attend_gossip_two_kernel(tc, query, keys_words, keys_scales, notes_word
             plane = sb.tile([P, width], U8, name=name, align_bytes=64)
             nc.vector.memset(plane[:].bitcast(I32), 0)
             for quad in range(4):
-                nc.scalar.dma_start(plane[32 * quad : 32 * quad + 4, :].bitcast(I32),
+                nc.sync.dma_start(plane[32 * quad : 32 * quad + 4, :].bitcast(I32),
                                     src[0, 4 * quad : 4 * quad + 4, :].bitcast(I32))
             return plane
 
         q_raw = sb.tile([P, PACK, Q], F32, name="q_raw")
         nc.sync.dma_start(q_raw[:], query.rearrange("(p j) q -> p j q", j=PACK))
         n_scales = load_scales("n_scales", notes_scales, U)
-        n_words = sb.tile([P, U], U32, name="n_words", align_bytes=64)
+        n_words = sb.tile([P, U], U32, name="n_words", tag="notes_then_f1", align_bytes=64)
         nc.sync.dma_start(n_words[:].bitcast(I32), notes_words[0].rearrange("p n t -> p (n t)").bitcast(I32))
         k_scales = load_scales("k_scales", keys_scales, T)
-        k_words = sb.tile([P, 2 * T], U8, name="k_words", align_bytes=64)
+        k_words = sb.tile([P, 2 * T], U8, name="k_words", tag="keys_then_f3", align_bytes=64)
         nc.sync.dma_start(k_words[:].bitcast(I32), keys_words[0].bitcast(I32))
         idx2 = load_list("idx2", offs2)
         idx = load_list("idx", offs)
@@ -66,11 +66,8 @@ def tile_attend_gossip_two_kernel(tc, query, keys_words, keys_scales, notes_word
         idx3 = load_list("idx3", offs3)
         idx5 = load_list("idx5", offs5)
 
-        f1 = sb.tile([P, T], F32, name="f1")
         f2 = sb.tile([P, U], F32, name="f2")
-        f3 = sb.tile([P, T], F32, name="f3")
         nc.vector.memset(f2[:], 0.0)
-        nc.vector.memset(f1[:], 0.0)
 
         q_bf = sb.tile([P, Q, PACK], BF16, name="q_bf", align_bytes=64)
         nc.vector.tensor_copy(q_bf[:], q_raw[:].rearrange("p j q -> p q j"))
@@ -78,7 +75,6 @@ def tile_attend_gossip_two_kernel(tc, query, keys_words, keys_scales, notes_word
         q_scales = sb.tile([P, Q], U8, name="q_scales", align_bytes=64)
         nc.vector.quantize_mx(out=q_codes[:].bitcast(FP8X4), scales=q_scales[:],
                               in_=q_bf[:].rearrange("p q j -> p (q j)"))
-        nc.vector.memset(f3[:], 0.0)
 
         def scores(name, words, scales, width):
             bank = psum.tile([P, width], F32, name=name)
@@ -89,46 +85,62 @@ def tile_attend_gossip_two_kernel(tc, query, keys_words, keys_scales, notes_word
         def key_scores(name, c0, c1):
             return scores(name, k_words[:, 2 * c0 : 2 * c1].bitcast(FP4X4), k_scales[:, c0:c1], c1 - c0)
 
+        def note_scores(name, c0, c1):
+            return scores(name, n_words[:, c0:c1].bitcast(FP8X4), n_scales[:, c0:c1], c1 - c0)
+
         a = sb.tile([P, T], F32, name="a")
         b = sb.tile([P, U], F32, name="b")
-        b0 = scores("b0", n_words[:, 0:BANK].bitcast(FP8X4), n_scales[:, 0:BANK], BANK)
-        b1 = scores("b1", n_words[:, BANK:U].bitcast(FP8X4), n_scales[:, BANK:U], BANK)
-        a0 = key_scores("a0", 0, 512)
-        a1 = key_scores("a1", 512, 768)
-        a2 = key_scores("a2", 768, 1024)
-        nc.scalar.copy(b[:, 0:BANK], b0[:])
-        nc.scalar.copy(b[:, BANK:U], b1[:])
-        nc.vector.tensor_copy(a[:, 0:512], a0[:])
-        gb = sb.tile([P, HALF], F32, name="gb")
-        nc.scalar.activation(gb[:], b[:].indirect(idx2[:, LIST_LO]), COPY)
-        nc.vector.tensor_copy(a[:, 512:768], a1[:])
-        nc.scalar.copy(a[:, 768:1024], a2[:])
+        b0 = note_scores("b0", 0, 512)
+        b1 = note_scores("b1", 512, 768)
+        b2 = note_scores("b2", 768, 1024)
+        a0 = key_scores("a0", 0, 256)
+        a1 = key_scores("a1", 256, 512)
+        a2 = key_scores("a2", 512, 768)
+        a3b = key_scores("a3b", 768, 1024)
+        f1 = sb.tile([P, T], F32, name="f1", tag="notes_then_f1", align_bytes=64)
+        f3 = sb.tile([P, T], F32, name="f3", tag="keys_then_f3", align_bytes=64)
+        nc.gpsimd.memset(f1[:], 0.0)
+        nc.gpsimd.memset(f3[:], 0.0)
+        nc.scalar.copy(b[:, 0:512], b0[:])
+        nc.vector.tensor_copy(b[:, 512:768], b1[:])
+        nc.scalar.copy(b[:, 768:1024], b2[:])
+        gb = sb.tile([P, SLOTS], F32, name="gb")
+        nc.scalar.activation(gb[:, LO], b[:].indirect(idx2[:, LIST_LO]), COPY)
+        nc.vector.tensor_copy(a[:, 0:256], a0[:])
+        nc.vector.tensor_copy(a[:, 256:512], a1[:])
+        nc.vector.tensor_copy(a[:, 512:768], a2[:])
+        nc.vector.tensor_copy(a[:, 768:1024], a3b[:])
+        nc.scalar.activation(gb[:, HI], b[:].indirect(idx2[:, LIST_HI]), COPY)
 
-        r_lo = sb.tile([P, HALF], F32, name="r_lo")
-        nc.vector.tensor_tensor(r_lo[:], a[:].indirect(idx[:, LIST_LO]), gb[:], SUB)
+        r = sb.tile([P, SLOTS], F32, name="r")
+        nc.vector.tensor_tensor(r[:, LO], a[:].indirect(idx[:, LIST_LO]), gb[:, LO], SUB)
         ga_hi = sb.tile([P, HALF], F32, name="ga_hi")
-        ngb_hi = sb.tile([P, HALF], F32, name="ngb_hi")
         nc.scalar.activation(ga_hi[:], a[:].indirect(idx[:, LIST_HI]), COPY)
-        nc.scalar.activation(ngb_hi[:], b[:].indirect(idx2[:, LIST_HI]), COPY, scale=-1.0)
+        nc.gpsimd.tensor_tensor(r[:, HI], ga_hi[:], gb[:, HI], SUB)
         neg_lam = sb.tile([P, 1], F32, name="neg_lam")
         nc.scalar.activation(neg_lam[:], lam_sb[:], COPY, scale=-1.0)
 
-        nc.vector.tensor_copy(f2[:].indirect(idx2[:, LIST_LO]), r_lo[:])
-        nc.vector.tensor_copy(f1[:].indirect(idx[:, LIST_LO]), r_lo[:])
-        nc.vector.tensor_tensor(f2[:].indirect(idx2[:, LIST_HI]), ga_hi[:], ngb_hi[:], ADD)
-        nc.vector.tensor_tensor(f1[:].indirect(idx[:, LIST_HI]), ga_hi[:], ngb_hi[:], ADD)
+        nc.vector.tensor_copy(f2[:].indirect(idx2[:, LIST_LO]), r[:, LO])
+        nc.vector.tensor_copy(f2[:].indirect(idx2[:, LIST_HI]), r[:, HI])
+        nc.vector.tensor_copy(f1[:].indirect(idx[:]), r[:])
 
         aa = sb.tile([P, T], F32, name="aa")
-        bb = sb.tile([P, U], F32, name="bb")
-        nc.vector.scalar_tensor_tensor(bb[:], f2[:], lam_sb[:], b[:], MULT, ADD)
+        bb = sb.tile([P, U], F32, name="bb", tag="bb_then_gaa")
+        step = sb.tile([P, U], F32, name="step")
+        for c in (slice(0, U // 2), slice(U // 2, U)):
+            nc.scalar.activation(step[:, c], f2[:, c], COPY, scale=lam_sb[:])
+            nc.gpsimd.tensor_tensor(bb[:, c], b[:, c], step[:, c], ADD)
         nc.vector.scalar_tensor_tensor(aa[:], f1[:], neg_lam[:], a[:], MULT, ADD)
 
         ngbb = sb.tile([P, SLOTS], F32, name="ngbb")
-        gaa = sb.tile([P, SLOTS], F32, name="gaa")
-        nc.scalar.activation(ngbb[:], bb[:].indirect(idx4[:]), COPY, scale=-1.0)
-        nc.vector.tensor_copy(gaa[:, LO], aa[:].indirect(idx3[:, LIST_LO]))
-        nc.scalar.activation(gaa[:, HI], aa[:].indirect(idx3[:, LIST_HI]), COPY)
-        nc.vector.tensor_tensor(f3[:].indirect(idx3[:]), gaa[:], ngbb[:], ADD)
+        gaa_lo = sb.tile([P, HALF], F32, name="gaa_lo")
+        nc.scalar.activation(ngbb[:, LO], bb[:].indirect(idx4[:, LIST_LO]), COPY, scale=-1.0)
+        nc.scalar.activation(ngbb[:, HI], bb[:].indirect(idx4[:, LIST_HI]), COPY, scale=-1.0)
+        nc.vector.tensor_copy(gaa_lo[:], aa[:].indirect(idx3[:, LIST_LO]))
+        gaa_hi = sb.tile([P, HALF], F32, name="gaa_hi", tag="bb_then_gaa")
+        nc.scalar.activation(gaa_hi[:], aa[:].indirect(idx3[:, LIST_HI]), COPY)
+        nc.vector.tensor_tensor(f3[:].indirect(idx3[:, LIST_LO]), gaa_lo[:], ngbb[:, LO], ADD)
+        nc.vector.tensor_tensor(f3[:].indirect(idx3[:, LIST_HI]), gaa_hi[:], ngbb[:, HI], ADD)
 
         a3 = sb.tile([P, T], F32, name="a3")
         nc.vector.scalar_tensor_tensor(a3[:], f3[:], neg_lam[:], aa[:], MULT, ADD)

@@ -42,22 +42,30 @@ def tile_attend_gossip_two_kernel(tc, query, keys_words, keys_scales, notes_word
             nc.sync.dma_start(tile[:], src)
             return tile
 
-        def load_scales(name, src, width):
+        def scale_plane(name, width):
             plane = sb.tile([P, width], U8, name=name, align_bytes=64)
             nc.vector.memset(plane[:].bitcast(I32), 0)
-            for quad in range(4):
-                nc.sync.dma_start(plane[32 * quad : 32 * quad + 4, :].bitcast(I32),
-                                    src[0, 4 * quad : 4 * quad + 4, :].bitcast(I32))
             return plane
+
+        def load_scales(plane, src, quads):
+            for quad in quads:
+                nc.sync.dma_start(plane[32 * quad : 32 * quad + 4, :].bitcast(I32),
+                                  src[0, 4 * quad : 4 * quad + 4, :].bitcast(I32))
 
         q_raw = sb.tile([P, PACK, Q], F32, name="q_raw")
         nc.sync.dma_start(q_raw[:], query.rearrange("(p j) q -> p j q", j=PACK))
-        n_scales = load_scales("n_scales", notes_scales, U)
-        n_words = sb.tile([P, U], U32, name="n_words", tag="notes_then_f1", align_bytes=64)
-        nc.sync.dma_start(n_words[:].bitcast(I32), notes_words[0].rearrange("p n t -> p (n t)").bitcast(I32))
-        k_scales = load_scales("k_scales", keys_scales, T)
+        n_scales = scale_plane("n_scales", U)
+        k_scales = scale_plane("k_scales", T)
+        notes_i32 = notes_words[0].rearrange("p n t -> p (n t)").bitcast(I32)
+        load_scales(n_scales, notes_scales, (0, 1, 2))
+        n_words0 = sb.tile([P, BANK], U32, name="n_words0", align_bytes=64)
+        nc.sync.dma_start(n_words0[:].bitcast(I32), notes_i32[:, 0:BANK])
+        load_scales(n_scales, notes_scales, (3,))
+        n_words1 = sb.tile([P, BANK], U32, name="n_words1", tag="notes_then_f1", align_bytes=64)
+        nc.sync.dma_start(n_words1[:].bitcast(I32), notes_i32[:, BANK:U])
         k_words = sb.tile([P, 2 * T], U8, name="k_words", tag="keys_then_f3", align_bytes=64)
         nc.sync.dma_start(k_words[:].bitcast(I32), keys_words[0].bitcast(I32))
+        load_scales(k_scales, keys_scales, (0, 1, 2, 3))
         idx2 = load_list("idx2", offs2)
         idx = load_list("idx", offs)
         lam_sb = sb.tile([P, 1], F32, name="lam_sb")
@@ -86,7 +94,8 @@ def tile_attend_gossip_two_kernel(tc, query, keys_words, keys_scales, notes_word
             return scores(name, k_words[:, 2 * c0 : 2 * c1].bitcast(FP4X4), k_scales[:, c0:c1], c1 - c0)
 
         def note_scores(name, c0, c1):
-            return scores(name, n_words[:, c0:c1].bitcast(FP8X4), n_scales[:, c0:c1], c1 - c0)
+            words = n_words0[:, c0:c1] if c1 <= BANK else n_words1[:, c0 - BANK : c1 - BANK]
+            return scores(name, words.bitcast(FP8X4), n_scales[:, c0:c1], c1 - c0)
 
         a = sb.tile([P, T], F32, name="a")
         b = sb.tile([P, U], F32, name="b")
@@ -121,16 +130,19 @@ def tile_attend_gossip_two_kernel(tc, query, keys_words, keys_scales, notes_word
         nc.scalar.activation(neg_lam[:], lam_sb[:], COPY, scale=-1.0)
 
         nc.vector.tensor_copy(f2[:].indirect(idx2[:, LIST_LO]), r[:, LO])
+        nc.vector.tensor_copy(f1[:].indirect(idx[:, 0:8]), r[:, 0:128])
         nc.vector.tensor_copy(f2[:].indirect(idx2[:, LIST_HI]), r[:, HI])
-        nc.vector.tensor_copy(f1[:].indirect(idx[:]), r[:])
+        nc.vector.tensor_copy(f1[:].indirect(idx[:, 8:LIST_COLS]), r[:, 128:SLOTS])
 
         aa = sb.tile([P, T], F32, name="aa")
         bb = sb.tile([P, U], F32, name="bb", tag="bb_then_gaa")
         step = sb.tile([P, U], F32, name="step")
-        for c in (slice(0, U // 2), slice(U // 2, U)):
+        for c in (slice(0, U // 4), slice(U // 4, U)):
             nc.scalar.activation(step[:, c], f2[:, c], COPY, scale=lam_sb[:])
             nc.gpsimd.tensor_tensor(bb[:, c], b[:, c], step[:, c], ADD)
-        nc.vector.scalar_tensor_tensor(aa[:], f1[:], neg_lam[:], a[:], MULT, ADD)
+        for n, bank in enumerate((a0, a1, a2, a3b)):
+            c = slice(256 * n, 256 * (n + 1))
+            nc.vector.scalar_tensor_tensor(aa[:, c], f1[:, c], neg_lam[:], bank[:], MULT, ADD)
 
         ngbb = sb.tile([P, SLOTS], F32, name="ngbb")
         gaa_lo = sb.tile([P, HALF], F32, name="gaa_lo")

@@ -136,10 +136,11 @@ def tile_attend_gossip_two_kernel(tc, query, keys_words, keys_scales, notes_word
 
         aa = sb.tile([P, T], F32, name="aa")
         bb = sb.tile([P, U], F32, name="bb", tag="bb_then_gaa")
-        step = sb.tile([P, U], F32, name="step")
-        for c in (slice(0, U // 4), slice(U // 4, U)):
+        step = sb.tile([P, 768], F32, name="step")
+        for c in (slice(0, 128), slice(128, 384), slice(384, 768)):
             nc.scalar.activation(step[:, c], f2[:, c], COPY, scale=lam_sb[:])
             nc.gpsimd.tensor_tensor(bb[:, c], b[:, c], step[:, c], ADD)
+        nc.vector.scalar_tensor_tensor(bb[:, 768:1024], f2[:, 768:1024], lam_sb[:], b2[:], MULT, ADD)
         for n, bank in enumerate((a0, a1, a2, a3b)):
             c = slice(256 * n, 256 * (n + 1))
             nc.vector.scalar_tensor_tensor(aa[:, c], f1[:, c], neg_lam[:], bank[:], MULT, ADD)

@@ -43,7 +43,7 @@ def tile_attend_gossip_two_kernel(tc, query, keys_words, keys_scales, notes_word
             return tile
 
         def scale_plane(name, width):
-            plane = sb.tile([P, width], U8, name=name, align_bytes=64)
+            plane = sb.tile([P, width], U8, name=name, tag=name, align_bytes=64)
             nc.vector.memset(plane[:].bitcast(I32), 0)
             return plane
 
@@ -78,11 +78,14 @@ def tile_attend_gossip_two_kernel(tc, query, keys_words, keys_scales, notes_word
         nc.vector.memset(f2[:], 0.0)
 
         q_bf = sb.tile([P, Q, PACK], BF16, name="q_bf", align_bytes=64)
-        nc.vector.tensor_copy(q_bf[:], q_raw[:].rearrange("p j q -> p q j"))
         q_codes = sb.tile([P, Q], U32, name="q_codes", align_bytes=64)
         q_scales = sb.tile([P, Q], U8, name="q_scales", align_bytes=64)
-        nc.vector.quantize_mx(out=q_codes[:].bitcast(FP8X4), scales=q_scales[:],
-                              in_=q_bf[:].rearrange("p q j -> p (q j)"))
+        halves = (slice(0, Q // 2), slice(Q // 2, Q))
+        for c in halves:
+            nc.vector.tensor_copy(q_bf[:, c, :], q_raw[:, :, c].rearrange("p j q -> p q j"))
+        for c in halves:
+            nc.vector.quantize_mx(out=q_codes[:, c].bitcast(FP8X4), scales=q_scales[:, c],
+                                  in_=q_bf[:, c, :].rearrange("p q j -> p (q j)"))
 
         def scores(name, words, scales, width):
             bank = psum.tile([P, width], F32, name=name)
@@ -105,7 +108,8 @@ def tile_attend_gossip_two_kernel(tc, query, keys_words, keys_scales, notes_word
         a0 = key_scores("a0", 0, 256)
         a1 = key_scores("a1", 256, 512)
         a2 = key_scores("a2", 512, 768)
-        a3b = key_scores("a3b", 768, 1024)
+        a3b = key_scores("a3b", 768, 896)
+        a4b = key_scores("a4b", 896, 1024)
         f1 = sb.tile([P, T], F32, name="f1", tag="notes_then_f1", align_bytes=64)
         f3 = sb.tile([P, T], F32, name="f3", tag="keys_then_f3", align_bytes=64)
         nc.gpsimd.memset(f1[:], 0.0)
@@ -113,19 +117,21 @@ def tile_attend_gossip_two_kernel(tc, query, keys_words, keys_scales, notes_word
         nc.scalar.copy(b[:, 0:512], b0[:])
         nc.vector.tensor_copy(b[:, 512:768], b1[:])
         nc.scalar.copy(b[:, 768:1024], b2[:])
-        gb = sb.tile([P, SLOTS], F32, name="gb")
-        nc.scalar.activation(gb[:, LO], b[:].indirect(idx2[:, LIST_LO]), COPY)
+        gb_lo = sb.tile([P, HALF], F32, name="gb_lo")
+        nc.scalar.activation(gb_lo[:], b[:].indirect(idx2[:, LIST_LO]), COPY)
         nc.vector.tensor_copy(a[:, 0:256], a0[:])
         nc.vector.tensor_copy(a[:, 256:512], a1[:])
         nc.vector.tensor_copy(a[:, 512:768], a2[:])
-        nc.vector.tensor_copy(a[:, 768:1024], a3b[:])
-        nc.scalar.activation(gb[:, HI], b[:].indirect(idx2[:, LIST_HI]), COPY)
+        nc.vector.tensor_copy(a[:, 768:896], a3b[:])
+        nc.scalar.copy(a[:, 896:1024], a4b[:])
+        gb_hi = sb.tile([P, HALF], F32, name="gb_hi", tag="k_scales", align_bytes=64)
+        nc.scalar.activation(gb_hi[:], b[:].indirect(idx2[:, LIST_HI]), COPY)
 
         r = sb.tile([P, SLOTS], F32, name="r")
-        nc.vector.tensor_tensor(r[:, LO], a[:].indirect(idx[:, LIST_LO]), gb[:, LO], SUB)
+        nc.vector.tensor_tensor(r[:, LO], a[:].indirect(idx[:, LIST_LO]), gb_lo[:], SUB)
         ga_hi = sb.tile([P, HALF], F32, name="ga_hi")
         nc.scalar.activation(ga_hi[:], a[:].indirect(idx[:, LIST_HI]), COPY)
-        nc.gpsimd.tensor_tensor(r[:, HI], ga_hi[:], gb[:, HI], SUB)
+        nc.gpsimd.tensor_tensor(r[:, HI], ga_hi[:], gb_hi[:], SUB)
         neg_lam = sb.tile([P, 1], F32, name="neg_lam")
         nc.scalar.activation(neg_lam[:], lam_sb[:], COPY, scale=-1.0)
 
@@ -141,9 +147,11 @@ def tile_attend_gossip_two_kernel(tc, query, keys_words, keys_scales, notes_word
             nc.scalar.activation(step[:, c], f2[:, c], COPY, scale=lam_sb[:])
             nc.gpsimd.tensor_tensor(bb[:, c], b[:, c], step[:, c], ADD)
         nc.vector.scalar_tensor_tensor(bb[:, 768:1024], f2[:, 768:1024], lam_sb[:], b2[:], MULT, ADD)
-        for n, bank in enumerate((a0, a1, a2, a3b)):
-            c = slice(256 * n, 256 * (n + 1))
-            nc.vector.scalar_tensor_tensor(aa[:, c], f1[:, c], neg_lam[:], bank[:], MULT, ADD)
+        for c0, c1, bank in ((0, 256, a0), (256, 512, a1), (512, 768, a2), (768, 896, a3b)):
+            nc.vector.scalar_tensor_tensor(aa[:, c0:c1], f1[:, c0:c1], neg_lam[:], bank[:], MULT, ADD)
+        step_a = sb.tile([P, 128], F32, name="step_a")
+        nc.scalar.activation(step_a[:], f1[:, 896:1024], COPY, scale=neg_lam[:])
+        nc.gpsimd.tensor_tensor(aa[:, 896:1024], a[:, 896:1024], step_a[:], ADD)
 
         ngbb = sb.tile([P, SLOTS], F32, name="ngbb")
         gaa_lo = sb.tile([P, HALF], F32, name="gaa_lo")

from contextlib import ExitStack

import concourse.mybir as mybir

D, T, U, SLOTS, Q = 512, 1024, 1024, 512, 128
FLOPS = 2 * D * Q * (T + U)

F32 = mybir.dt.float32
BF16 = mybir.dt.bfloat16
I32 = mybir.dt.int32
U32 = mybir.dt.uint32
U16 = mybir.dt.uint16
U8 = mybir.dt.uint8
FP8X4 = mybir.dt.float8_e4m3fn_x4
FP4X4 = mybir.dt.float4_e2m1fn_x4
MULT = mybir.AluOpType.mult
ADD = mybir.AluOpType.add
SUB = mybir.AluOpType.subtract
COPY = mybir.ActivationFunctionType.Copy

P = 128
PACK = 4
BANK = 512
HALF = SLOTS // 2
LIST_COLS = SLOTS // 16
LO = slice(0, HALF)
HI = slice(HALF, SLOTS)
LIST_LO = slice(0, LIST_COLS // 2)
LIST_HI = slice(LIST_COLS // 2, LIST_COLS)


def tile_attend_gossip_two_kernel(tc, query, keys_words, keys_scales, notes_words, notes_scales, lam,
                                   offs, offs2, offs3, offs4, offs5, out):
    nc = tc.nc
    with ExitStack() as ctx:
        lists = ctx.enter_context(tc.tile_pool(name="lists", bufs=1))
        sb = ctx.enter_context(tc.tile_pool(name="sb", bufs=1))
        psum = ctx.enter_context(tc.psum_pool(name="psum", bufs=1))

        def load_list(name, src):
            tile = lists.tile([P, LIST_COLS], U16, name=name)
            nc.sync.dma_start(tile[:], src)
            return tile

        def scale_plane(name, width):
            plane = sb.tile([P, width], U8, name=name, tag=name, align_bytes=64)
            nc.vector.memset(plane[:].bitcast(I32), 0)
            return plane

        def load_scales(plane, src, quads):
            for quad in quads:
                nc.sync.dma_start(plane[32 * quad : 32 * quad + 4, :].bitcast(I32),
                                  src[0, 4 * quad : 4 * quad + 4, :].bitcast(I32))

        q_raw = sb.tile([P, PACK, Q], F32, name="q_raw")
        nc.sync.dma_start(q_raw[:], query.rearrange("(p j) q -> p j q", j=PACK))
        n_scales = scale_plane("n_scales", U)
        k_scales = scale_plane("k_scales", T)
        notes_i32 = notes_words[0].rearrange("p n t -> p (n t)").bitcast(I32)
        load_scales(n_scales, notes_scales, (0, 1, 2))
        n_words0 = sb.tile([P, BANK], U32, name="n_words0", align_bytes=64)
        nc.sync.dma_start(n_words0[:].bitcast(I32), notes_i32[:, 0:BANK])
        load_scales(n_scales, notes_scales, (3,))
        n_words1 = sb.tile([P, BANK], U32, name="n_words1", tag="notes_then_f1", align_bytes=64)
        nc.sync.dma_start(n_words1[:].bitcast(I32), notes_i32[:, BANK:U])
        k_words = sb.tile([P, 2 * T], U8, name="k_words", tag="keys_then_f3", align_bytes=64)
        nc.sync.dma_start(k_words[:].bitcast(I32), keys_words[0].bitcast(I32))
        load_scales(k_scales, keys_scales, (0, 1, 2, 3))
        idx2 = load_list("idx2", offs2)
        idx = load_list("idx", offs)
        lam_sb = sb.tile([P, 1], F32, name="lam_sb")
        nc.sync.dma_start(lam_sb[:], lam)
        idx4 = load_list("idx4", offs4)
        idx3 = load_list("idx3", offs3)
        idx5 = load_list("idx5", offs5)

        f2 = sb.tile([P, U], F32, name="f2")
        nc.vector.memset(f2[:], 0.0)

        q_bf = sb.tile([P, Q, PACK], BF16, name="q_bf", align_bytes=64)
        q_codes = sb.tile([P, Q], U32, name="q_codes", align_bytes=64)
        q_scales = sb.tile([P, Q], U8, name="q_scales", align_bytes=64)
        halves = (slice(0, Q // 2), slice(Q // 2, Q))
        for c in halves:
            nc.vector.tensor_copy(q_bf[:, c, :], q_raw[:, :, c].rearrange("p j q -> p q j"))
        for c in halves:
            nc.vector.quantize_mx(out=q_codes[:, c].bitcast(FP8X4), scales=q_scales[:, c],
                                  in_=q_bf[:, c, :].rearrange("p q j -> p (q j)"))

        def scores(name, words, scales, width):
            bank = psum.tile([P, width], F32, name=name)
            nc.tensor.matmul_mx(out=bank[:], lhsT=q_codes[:].bitcast(FP8X4), lhsT_scale=q_scales[:],
                                rhs=words, rhs_scale=scales, start=True, stop=True)
            return bank

        def key_scores(name, c0, c1):
            return scores(name, k_words[:, 2 * c0 : 2 * c1].bitcast(FP4X4), k_scales[:, c0:c1], c1 - c0)

        def note_scores(name, c0, c1):
            words = n_words0[:, c0:c1] if c1 <= BANK else n_words1[:, c0 - BANK : c1 - BANK]
            return scores(name, words.bitcast(FP8X4), n_scales[:, c0:c1], c1 - c0)

        a = sb.tile([P, T], F32, name="a")
        b = sb.tile([P, U], F32, name="b")
        b0 = note_scores("b0", 0, 512)
        b1 = note_scores("b1", 512, 768)
        b2 = note_scores("b2", 768, 1024)
        a0 = key_scores("a0", 0, 256)
        a1 = key_scores("a1", 256, 512)
        a2 = key_scores("a2", 512, 768)
        a3b = key_scores("a3b", 768, 896)
        a4b = key_scores("a4b", 896, 1024)
        f1 = sb.tile([P, T], F32, name="f1", tag="notes_then_f1", align_bytes=64)
        f3 = sb.tile([P, T], F32, name="f3", tag="keys_then_f3", align_bytes=64)
        nc.gpsimd.memset(f1[:], 0.0)
        nc.gpsimd.memset(f3[:], 0.0)
        nc.scalar.copy(b[:, 0:512], b0[:])
        nc.vector.tensor_copy(b[:, 512:768], b1[:])
        nc.scalar.copy(b[:, 768:1024], b2[:])
        gb_lo = sb.tile([P, HALF], F32, name="gb_lo")
        nc.scalar.activation(gb_lo[:], b[:].indirect(idx2[:, LIST_LO]), COPY)
        nc.vector.tensor_copy(a[:, 0:256], a0[:])
        nc.vector.tensor_copy(a[:, 256:512], a1[:])
        nc.vector.tensor_copy(a[:, 512:768], a2[:])
        nc.vector.tensor_copy(a[:, 768:896], a3b[:])
        nc.scalar.copy(a[:, 896:1024], a4b[:])
        gb_hi = sb.tile([P, HALF], F32, name="gb_hi", tag="k_scales", align_bytes=64)
        nc.scalar.activation(gb_hi[:], b[:].indirect(idx2[:, LIST_HI]), COPY)

        r = sb.tile([P, SLOTS], F32, name="r")
        nc.vector.tensor_tensor(r[:, LO], a[:].indirect(idx[:, LIST_LO]), gb_lo[:], SUB)
        ga_hi = sb.tile([P, HALF], F32, name="ga_hi")
        nc.scalar.activation(ga_hi[:], a[:].indirect(idx[:, LIST_HI]), COPY)
        nc.gpsimd.tensor_tensor(r[:, HI], ga_hi[:], gb_hi[:], SUB)
        neg_lam = sb.tile([P, 1], F32, name="neg_lam")
        nc.scalar.activation(neg_lam[:], lam_sb[:], COPY, scale=-1.0)

        nc.vector.tensor_copy(f2[:].indirect(idx2[:, LIST_LO]), r[:, LO])
        nc.vector.tensor_copy(f1[:].indirect(idx[:, 0:8]), r[:, 0:128])
        nc.vector.tensor_copy(f2[:].indirect(idx2[:, LIST_HI]), r[:, HI])
        nc.vector.tensor_copy(f1[:].indirect(idx[:, 8:LIST_COLS]), r[:, 128:SLOTS])

        aa = sb.tile([P, T], F32, name="aa")
        bb = sb.tile([P, U], F32, name="bb", tag="bb_then_gaa")
        step = sb.tile([P, 768], F32, name="step")
        for c in (slice(0, 128), slice(128, 384), slice(384, 768)):
            nc.scalar.activation(step[:, c], f2[:, c], COPY, scale=lam_sb[:])
            nc.gpsimd.tensor_tensor(bb[:, c], b[:, c], step[:, c], ADD)
        nc.vector.scalar_tensor_tensor(bb[:, 768:1024], f2[:, 768:1024], lam_sb[:], b2[:], MULT, ADD)
        for c0, c1, bank in ((0, 256, a0), (256, 512, a1), (512, 768, a2), (768, 896, a3b)):
            nc.vector.scalar_tensor_tensor(aa[:, c0:c1], f1[:, c0:c1], neg_lam[:], bank[:], MULT, ADD)
        step_a = sb.tile([P, 128], F32, name="step_a")
        nc.scalar.activation(step_a[:], f1[:, 896:1024], COPY, scale=neg_lam[:])
        nc.gpsimd.tensor_tensor(aa[:, 896:1024], a[:, 896:1024], step_a[:], ADD)

        ngbb = sb.tile([P, SLOTS], F32, name="ngbb")
        gaa_lo = sb.tile([P, HALF], F32, name="gaa_lo")
        nc.scalar.activation(ngbb[:, LO], bb[:].indirect(idx4[:, LIST_LO]), COPY, scale=-1.0)
        nc.scalar.activation(ngbb[:, HI], bb[:].indirect(idx4[:, LIST_HI]), COPY, scale=-1.0)
        nc.vector.tensor_copy(gaa_lo[:], aa[:].indirect(idx3[:, LIST_LO]))
        gaa_hi = sb.tile([P, HALF], F32, name="gaa_hi", tag="bb_then_gaa")
        nc.scalar.activation(gaa_hi[:], aa[:].indirect(idx3[:, LIST_HI]), COPY)
        nc.vector.tensor_tensor(f3[:].indirect(idx3[:, LIST_LO]), gaa_lo[:], ngbb[:, LO], ADD)
        nc.vector.tensor_tensor(f3[:].indirect(idx3[:, LIST_HI]), gaa_hi[:], ngbb[:, HI], ADD)

        a3 = sb.tile([P, T], F32, name="a3")
        nc.vector.scalar_tensor_tensor(a3[:], f3[:], neg_lam[:], aa[:], MULT, ADD)
        y_lo = sb.tile([P, HALF], F32, name="y_lo")
        y_hi = sb.tile([P, HALF], F32, name="y_hi")
        nc.vector.tensor_copy(y_lo[:], a3[:].indirect(idx5[:, LIST_LO]))
        nc.scalar.activation(y_hi[:], a3[:].indirect(idx5[:, LIST_HI]), COPY)
        nc.sync.dma_start(out[:, LO], y_lo[:])
        nc.scalar.dma_start(out[:, HI], y_hi[:])
